import numpy as np, ml_dtypes
CORES = [5,21,45,77,85,101,109,125,133,141,189,213]
N = 12
import mx_ref
NC = 128
BF = ml_dtypes.bfloat16
def cut(t, i, w=512):
    return t[:, w * i:w * i + w]
def pk(c, s, i=0):
    return (np.ascontiguousarray(c[:, 512 * i:512 * i + 512]), mx_ref.live(s[:, 128 * i:128 * i + 128]))
def inputs(rng, e, E):
    def f(*shape):
        v = (rng.standard_normal(shape, dtype=np.float32) * np.exp2(rng.integers(-2, 3, shape[:-1] + (1,)))).astype(BF)
        return mx_ref.spread((v.astype(np.float32) * np.exp2(rng.integers(-E, E + 1, shape[:-2] + (1, 1))).astype(np.float32)).astype(BF), rng, e)
    def packed(k):
        c = np.zeros((N, 128, k * 512), np.uint8); s = np.zeros((N, 128, k * 128), np.uint8)
        for r in range(N):
            for i in range(k):
                a, b = mx_ref.quantize(f(128, 512)); c[r][:, 512 * i:512 * i + 512] = a; s[r][:, 128 * i:128 * i + 128] = mx_ref.plane(b, rng)
        return c, s
    d = {}
    d["wc"], d["ws"] = packed(N)
    d["x"] = f(N, 128, 4 * NC)
    return d
def setup_inputs(rng):
    return inputs(rng, 0, 0)
def setup_inputs_blocks(rng):
    return inputs(rng, 4, 0)
def setup_inputs_wide(rng):
    return inputs(rng, 0, 8)
def reference(wc, ws, x):
    y = np.zeros((N, 128, N * NC), np.float32)
    for r in range(N):
        X = mx_ref.quantize(x[r])
        for j in range(N):
            y[r][:, NC * j:NC * j + NC] = mx_ref.matmul(pk(wc[j], ws[j], r), X)
    return {"y": y}

from concourse.bass import DstId, RemoteDMATransfer
from concourse.mybir import dt, ActivationFunctionType

N = 12
W = 128
WORLD = 256
NPH = 3
PT = N // NPH
NQ = N // 2
BANKS = 8

SCRATCH = {
    "wq": ("sbuf", [128, N * W], "float8_e4m3fn_x4"),
    "wp": ("sbuf", [128, N * W], "uint8"),
    "lq": ("sbuf", [128, N * W], "float8_e4m3fn_x4"),
    "lp": ("sbuf", [128, N * W], "uint8"),
    "xb": ("sbuf", [128, 4 * W], "bfloat16"),
    "xq": ("sbuf", [128, W], "float8_e4m3fn_x4"),
    "xp": ("sbuf", [128, W], "uint8"),
    "yb": ("sbuf", [128, N * W], "float32"),
    "ps": ("psum", [128, BANKS * 512], "float32"),
}
SEMAPHORES = (["ldp", "ldx", "hs", "hc", "sent", "xqd", "st"] + ["ldc%d" % k for k in range(NPH)]
              + ["arr%d" % j for j in range(N)] + ["mm%d" % j for j in range(N)] + ["cp%d" % j for j in range(N)])

_CACHE = {}


def _engines(mask):
    return [e for e in range(mask.bit_length()) if (mask >> e) & 1]


def _mask(engs):
    m = 0
    for e in engs:
        m |= 1 << e
    return m


def _phase(s, t):
    return (t // PT - (s // 2) % NPH) % NPH


def _step(s, t):
    return (t + (s // 2) // NPH) % 2


def _dests(s, q):
    return sorted([t for t in (2 * q, 2 * q + 1) if t != s], key=lambda t: _step(s, t))


def _assign(pairs, cands, ok):
    if not pairs:
        return []
    for i, c in enumerate(cands):
        if ok(c, pairs[0]):
            rest = _assign(pairs[1:], cands[:i] + cands[i + 1:], ok)
            if rest is not None:
                return [c] + rest
    return None


def _plan(cores, topo):
    if "plan" in _CACHE:
        return _CACHE["plan"]
    for code in range(2 ** NPH):
        pat = []
        for p in range(NPH):
            pat += [(code >> p) & 1, 1 - ((code >> p) & 1)]
        helper = {}
        for s, S in enumerate(cores):
            chip = [c for c in range(WORLD) if c not in cores
                    and topo.host(c) == topo.host(S) and topo.chip(c) == topo.chip(S)]
            dies = sorted(set([topo.die(c) for c in chip]))

            def ok(c, q):
                return all(topo.may_write(c, cores[t]) for t in _dests(s, q))
            for d in range(2):
                qs = [q for q in range(NQ) if (s % 2) ^ pat[q] == d]
                got = _assign(qs, [c for c in chip if topo.die(c) == dies[d]], ok)
                if got is None:
                    helper = None
                    break
                for q, c in zip(qs, got):
                    helper[(s, q)] = c
            if helper is None:
                break
        if helper is not None:
            role = {}
            for k in helper:
                role[helper[k]] = k
            _CACHE["plan"] = (helper, role)
            return _CACHE["plan"]
    return None


def _share(core, helpers, topo):
    m = topo.mask(core, helpers[0])
    for h in helpers:
        m &= topo.mask(core, h)
    engs = _engines(m)
    out = {}
    near = [h for h in helpers if topo.die(h) == topo.die(core)]
    far = [h for h in helpers if topo.die(h) != topo.die(core)]
    for grp, es in ((near, engs[0::2]), (far, engs[1::2])):
        n = len(es) // len(grp)
        for i, h in enumerate(grp):
            out[h] = es[i * n:(i + 1) * n]
    return out


def _out_engines(core, cores, dests, topo):
    m = topo.mask(core, cores[dests[0]])
    for t in dests:
        m &= topo.mask(core, cores[t])
    return _engines(m)


def _xfer(topo, src_core, dst_core, engs, sem, src, dst):
    rid, pid = topo.addr(dst_core, src_core)
    return RemoteDMATransfer(dst_ids=[DstId(rid=rid, pnc=pid)], dma_engine_mask=_mask(engs), remote_sem=sem,
                             src=src, dst=dst)


def _codes(buf, a, b):
    return buf[:, a * W:b * W].bitcast(dt.uint8)


def _plane(buf, a, b):
    return buf[:, a * W:b * W]


def _hs_groups():
    return [[0], list(range(1, NPH))]


def _helper_program(g, core, T, topo, s, q):
    cores, S = T.cores, T.sem
    dests = _dests(s, q)
    engs = _out_engines(core, cores, dests, topo)
    k = _phase(s, 2 * q)
    for grp in _hs_groups():
        if k in grp:
            n_hs = len(_engines(topo.mask(cores[s], core))) // (2 * len(grp))
    n_hc = len(_engines(topo.mask(cores[s], core))) // 2
    arr = S["arr%d" % s]
    sent = 0
    g.wait_ge(S.hs, n_hs)
    n = len(engs) // len(dests)
    g.remote_dma_fused([_xfer(topo, core, cores[t], engs[i::len(dests)], arr, _plane(T.lp, t, t + 1), _plane(T.lp, s, s + 1))
                        for i, t in enumerate(dests)], local_sem=S.sent)
    sent += n * len(dests)
    g.wait_ge(S.hc, n_hc)
    for t in dests:
        rid, pid = topo.addr(cores[t], core)
        g.remote_dma(_codes(T.lq, s, s + 1), _codes(T.lq, t, t + 1), arr, S.sent, pid, rid, _mask(engs))
        sent += len(engs)
    g.wait_ge(S.sent, sent)


def _rank_program(g, core, T, topo, r, helper):
    cores, S = T.cores, T.sem
    pieces = [((r // 2) % NPH + k) % NPH for k in range(NPH)]

    def load_piece(queue, k):
        p = pieces[k]
        queue.dma_start(_codes(T.wq, p * PT, (p + 1) * PT), T.wc[:, p * PT * 4 * W:(p + 1) * PT * 4 * W]).then_inc(S["ldc%d" % k], 16)
    g.sync.dma_start(T.wp[:], T.ws[:]).then_inc(S.ldp, 16)
    load_piece(g.scalar, 0)
    load_piece(g.sync, 1)
    load_piece(g.scalar, 2)
    g.sync.dma_start(T.xb[:], T.x[:]).then_inc(S.ldx, 16)

    def pairs_of(k):
        return [pieces[k] * PT // 2 + i for i in range(PT // 2)]
    sent = 0
    g.wait_ge(S.ldp, 16)
    for grp in _hs_groups():
        qs = [q for k in grp for q in pairs_of(k)]
        share = _share(core, [helper[(r, q)] for q in qs], topo)
        g.remote_dma_fused([_xfer(topo, core, helper[(r, q)], share[helper[(r, q)]], S.hs,
                                  _plane(T.wp, 2 * q, 2 * q + 2), _plane(T.lp, 2 * q, 2 * q + 2)) for q in qs],
                           local_sem=S.sent)
        sent += sum(len(share[helper[(r, q)]]) for q in qs)
    for k in range(NPH):
        qs = pairs_of(k)
        share = _share(core, [helper[(r, q)] for q in qs], topo)
        g.wait_ge(S["ldc%d" % k], 16)
        g.remote_dma_fused([_xfer(topo, core, helper[(r, q)], share[helper[(r, q)]], S.hc,
                                  _codes(T.wq, 2 * q, 2 * q + 2), _codes(T.lq, 2 * q, 2 * q + 2)) for q in qs],
                           local_sem=S.sent)
        sent += sum(len(share[helper[(r, q)]]) for q in qs)
    g.wait_ge(S.sent, sent)

    g.vector.wait_ge(S.ldx, 16)
    g.vector.quantize_mx(T.xq[:], T.xp[:], T.xb[:]).then_inc(S.xqd, 1)

    waves = sorted(range(NQ), key=lambda u: 2 * _phase(2 * u, r) + _step(2 * u, r))
    order = [r] + [j for u in waves for j in (2 * u, 2 * u + 1) if j != r]
    g.tensor.wait_ge(S.xqd, 1)
    for i, j in enumerate(order):
        if j == r:
            g.tensor.wait_ge(S.ldp, 16)
            g.tensor.wait_ge(S["ldc%d" % _phase(r, r)], 16)
            cq, cp = T.wq, T.wp
        else:
            q = r // 2
            dests = _dests(j, q)
            n = len(_out_engines(helper[(j, q)], cores, dests, topo))
            g.tensor.wait_ge(S["arr%d" % j], n // len(dests) + n)
            cq, cp = T.lq, T.lp
        if i >= BANKS:
            g.tensor.wait_ge(S["cp%d" % order[i - BANKS]], 1)
        bank = T.ps[:, (i % BANKS) * 512:(i % BANKS) * 512 + W]
        g.tensor.matmul_mx(bank, cq[:, j * W:(j + 1) * W], cp[:, j * W:(j + 1) * W], T.xq[:], T.xp[:], True, True).then_inc(S["mm%d" % j], 1)
        out = T.yb[:, j * W:(j + 1) * W]
        if i % 2 == 0:
            g.vector.wait_ge(S["mm%d" % j], 1)
            g.vector.tensor_copy(out, bank).then_inc(S["cp%d" % j], 1)
        else:
            g.scalar.wait_ge(S["mm%d" % j], 1)
            g.scalar.activation(out, bank, ActivationFunctionType.Copy).then_inc(S["cp%d" % j], 1)

    for u in waves:
        g.sync.wait_ge(S["cp%d" % (2 * u)], 1)
        g.sync.wait_ge(S["cp%d" % (2 * u + 1)], 1)
        g.sync.dma_start(T.y[:, 2 * u * W:(2 * u + 2) * W], T.yb[:, 2 * u * W:(2 * u + 2) * W]).then_inc(S.st, 16)
    g.sync.wait_ge(S.st, 16 * NQ)


def rank_program(g, core, T, topo):
    helper, role = _plan(list(T.cores), topo)
    r = T.rank_of(core)
    if r is not None:
        _rank_program(g, core, T, topo, r, helper)
    elif core in role:
        s, q = role[core]
        _helper_program(g, core, T, topo, s, q)
